import numpy as np, ml_dtypes
CORES = [9,10,11,14,17,18,19,22,49,50,51,54]
N = 12
TK = 32
def setup_inputs(rng):
    return {"x": rng.standard_normal((N, 128, TK), dtype=np.float32).astype(ml_dtypes.bfloat16), "w": rng.standard_normal((N, 128, 128), dtype=np.float32).astype(ml_dtypes.bfloat16)}
def setup_inputs_big(rng):
    d = setup_inputs(rng)
    for k in ("x", "w"): d[k] = (d[k].astype(np.float32) * 1024.0).astype(d[k].dtype)
    return d
def setup_inputs_small(rng):
    d = setup_inputs(rng)
    for k in ("x", "w"): d[k] = (d[k].astype(np.float32) * (1 / 1024.0)).astype(d[k].dtype)
    return d
def setup_inputs_apart(rng):
    d = setup_inputs(rng)
    f = (10.0 ** rng.permutation(np.linspace(-1.5, 1.5, N))).astype(np.float32).reshape(N, 1, 1)
    for k in ("x", "w"): d[k] = (d[k].astype(np.float32) * f).astype(d[k].dtype)
    return d
def setup_inputs_neg(rng):
    d = setup_inputs(rng)
    d["x"] = (np.abs(d["x"].astype(np.float32)) * 1048576.0).astype(d["x"].dtype); d["w"] = (-np.abs(d["w"].astype(np.float32))).astype(d["w"].dtype)
    return d
def reference(x, w):
    X, W = x.astype(np.float64), w.astype(np.float64)
    y = np.stack([np.max([W[j].T @ X[r] for j in range(N)], axis=0) for r in range(N)])
    return {"y": y.astype(ml_dtypes.bfloat16)}

@@ -1,0 +1,252 @@
+from concourse.bass import DstId, RemoteDMATransfer
+from concourse.mybir import AluOpType
+
+TK = 32
+D = 128
+
+SCRATCH = {
+    "W": ("sbuf", [128, 4 * D], "bfloat16"),
+    "X": ("sbuf", [128, 8 * TK], "bfloat16"),
+    "ps1": ("psum", [128, 512], "float32"),
+    "ps2": ("psum", [128, 512], "float32"),
+    "ps3": ("psum", [128, 512], "float32"),
+    "ta1": ("sbuf", [128, 256], "float32"),
+    "tb1": ("sbuf", [128, 256], "float32"),
+    "ta2": ("sbuf", [128, 256], "float32"),
+    "tb2": ("sbuf", [128, 256], "float32"),
+    "ta3": ("sbuf", [128, 256], "float32"),
+    "tb3": ("sbuf", [128, 256], "float32"),
+    "P1": ("sbuf", [128, 4 * TK], "bfloat16"),
+    "P2": ("sbuf", [128, 4 * TK], "bfloat16"),
+    "P3": ("sbuf", [128, TK], "bfloat16"),
+    "LAND": ("sbuf", [128, 4 * TK], "bfloat16"),
+    "TT": ("sbuf", [128, 4 * TK], "bfloat16"),
+    "Y": ("sbuf", [128, TK], "bfloat16"),
+}
+SEMAPHORES = ["xl", "wl", "wa", "xr", "xa1", "xa2", "mm1", "mm2", "mm3", "v1", "v2", "v3",
+              "ra0", "ra1", "ra2", "ra3", "vf", "st", "ls"]
+
+
+def _bits(mask):
+    return [i for i in range(mask.bit_length()) if (mask >> i) & 1]
+
+
+def _mask(bits):
+    m = 0
+    for b in bits:
+        m |= 1 << b
+    return m
+
+
+def _split(bits, n):
+    k = 1
+    while 2 * k * n <= len(bits):
+        k *= 2
+    return [bits[i * k:(i + 1) * k] for i in range(n)]
+
+
+def _plan(cores, topo):
+    chip = topo.chip
+    chips = []
+    for c in cores:
+        if chip(c) not in chips:
+            chips.append(chip(c))
+    mem = {ch: [c for c in cores if chip(c) == ch] for ch in chips}
+    hosts = {ch: [m for m in mem[ch] if any(topo.may_write(m, r) for r in cores if chip(r) != ch)] for ch in chips}
+    load = {c: 0 for c in cores}
+    nlate = {c: 0 for c in cores}
+    host, late = {}, {}
+    for ch in chips:
+        todo = []
+        for i, r in enumerate(cores):
+            if chip(r) == ch:
+                continue
+            back = [h for h in hosts[ch] if topo.may_write(h, r)]
+            direct = [h for h in back if topo.may_write(r, h)]
+            todo.append((1 if direct else 0, len(direct or back), i, r, direct or back))
+        for early, _n, _i, r, cand in sorted(todo):
+            h = min(cand, key=lambda c: (0 if early else nlate[c], load[c], cores.index(c)))
+            host[(r, ch)] = h
+            late[(r, ch)] = not early
+            load[h] += 1
+            nlate[h] += 0 if early else 1
+    for r in cores:
+        ch = chip(r)
+        host[(r, ch)] = r if r in hosts[ch] else min(hosts[ch], key=lambda c: (load[c], cores.index(c)))
+        late[(r, ch)] = False
+    via = {}
+    for (r, ch), is_late in sorted(late.items()):
+        if not is_late:
+            continue
+        h, home = host[(r, ch)], host[(r, chip(r))]
+        cand = [q for q in mem[chip(r)] if q != r and topo.may_write(q, h)]
+        q = home if home in cand else min(cand, key=lambda c: (nlate[c], load[c], cores.index(c)))
+        via[(r, ch)] = q
+        load[q] += 1
+    wave1 = {c: [] for c in cores}
+    wave2 = {c: [] for c in cores}
+    relay = {c: {} for c in cores}
+    xdst = {c: [] for c in cores}
+    for r in cores:
+        for ch in chips:
+            q = via.get((r, ch))
+            if q is not None:
+                relay[q].setdefault(r, []).append(host[(r, ch)])
+                wave2[host[(r, ch)]].append(r)
+                if q not in xdst[r]:
+                    xdst[r].append(q)
+        for ch in chips:
+            h = host[(r, ch)]
+            if (r, ch) not in via and h != r:
+                wave1[h].append(r)
+                if h not in xdst[r]:
+                    xdst[r].append(h)
+    col = {}
+    for c in cores:
+        order = wave1[c] + wave2[c] + [c] + [r for r in relay[c] if r not in wave1[c]]
+        col[c] = {r: k for k, r in enumerate(order)}
+    lands = {r: [host[(r, chip(r))]] * (host[(r, chip(r))] != r) + [host[(r, ch)] for ch in chips if ch != chip(r)]
+             for r in cores}
+    needs = {r: any((r, ch) in via for ch in chips) for r in cores}
+    offb, onb, xbits, wbits, wdst, ret = {}, {}, {}, {}, {}, {}
+    for c in cores:
+        far = [o for o in cores if chip(o) != chip(c)][0]
+        near = [o for o in mem[chip(c)] if o != c][0]
+        offb[c] = _bits(topo.mask(c, far))
+        onb[c] = [b for b in _bits(topo.mask(c, near)) if b not in offb[c]]
+        xbits[c] = offb[c]
+        wbits[c] = (offb[c] + onb[c]) if needs[c] else (onb[c] or offb[c])
+        wdst[c] = [h for h in hosts[chip(c)] if h != c]
+        ret[c] = []
+        for wave in (wave1[c], wave2[c]):
+            off = [r for r in wave if chip(r) != chip(c)]
+            on = [r for r in wave if chip(r) == chip(c)]
+            eng = dict(zip(off, _split(offb[c], max(1, len(off)))))
+            eng.update(zip(on, _split(onb[c] or offb[c], max(1, len(on)))))
+            ret[c].append([(r, eng[r]) for r in wave])
+    return dict(mem=mem, hosts=hosts, wave1=wave1, wave2=wave2, relay=relay, xdst=xdst, col=col, lands=lands,
+                needs=needs, xbits=xbits, wbits=wbits, wdst=wdst, ret=ret)
+
+
+def rank_program(g, core, T, topo):
+    if T.rank_of(core) is None:
+        return
+    cores = list(T.cores)
+    P = _plan(cores, topo)
+    S = T.sem
+    mem = P["mem"][topo.chip(core)]
+    nm = len(mem)
+    is_host = core in P["hosts"][topo.chip(core)]
+    sent = [0]
+
+    def xslot(c, r):
+        k = P["col"][c][r]
+        return T.X[:, k * TK:(k + 1) * TK]
+
+    def wslot(m):
+        k = mem.index(m)
+        return T.W[:, k * D:(k + 1) * D]
+
+    def ident(c):
+        rid, pid, _se = topo.addr(c)
+        return DstId(rid=rid, pnc=pid)
+
+    def fused(items):
+        trs = []
+        for src, dl, bits, sem in items:
+            trs.append(RemoteDMATransfer(dst_ids=[ident(c) for c, _a in dl], dma_engine_mask=_mask(bits),
+                                         remote_sem=sem, srcs=[src], dsts=[a for _c, a in dl], alu_op=0))
+            sent[0] += len(bits)
+        g.remote_dma_fused(trs, local_sem=S.ls)
+
+    g.sync.dma_start(xslot(core, core), T.x[:, :]).then_inc(S.xl, 16)
+    g.scalar.dma_start(wslot(core), T.w[:, :]).then_inc(S.wl, 16)
+
+    n_wa = sum(len(P["wbits"][m]) for m in mem if m != core) if is_host else 0
+    n_xr = sum(len(P["xbits"][s]) for s in cores if P["needs"][s] and core in P["xdst"][s])
+    n_xa1 = sum(len(P["xbits"][s]) for s in cores if not P["needs"][s] and core in P["xdst"][s])
+    n_xa2 = sum(len(P["xbits"][q]) for q in cores for r, hs in P["relay"][q].items() if core in hs)
+
+    def send_x():
+        g.wait_ge(S.xl, 16)
+        fused([(xslot(core, core), [(c, xslot(c, core)) for c in P["xdst"][core]], P["xbits"][core],
+                S.xr if P["needs"][core] else S.xa1)])
+
+    def send_w():
+        g.wait_ge(S.wl, 16)
+        fused([(wslot(core), [(c, wslot(core)) for c in P["wdst"][core]], P["wbits"][core], S.wa)])
+
+    x_rows = len(P["xdst"][core]) / len(P["xbits"][core])
+    w_rows = len(P["wdst"][core]) / len(P["wbits"][core])
+    if P["needs"][core] or x_rows >= w_rows:
+        send_x()
+        send_w()
+    else:
+        send_w()
+        send_x()
+    if P["relay"][core]:
+        g.wait_ge(S.xr, n_xr)
+        for r, hs in P["relay"][core].items():
+            fused([(xslot(core, r), [(h, xslot(h, r)) for h in hs], P["xbits"][core], S.xa2)])
+
+    waves = []
+    if is_host:
+        waves = [(1, P["wave1"][core]), (2, P["wave2"][core]), (3, [core])]
+    first = True
+    for k, wave in waves:
+        if not wave:
+            continue
+        wd = TK * len(wave)
+        c0 = P["col"][core][wave[0]] * TK
+        ps, ta, tb, out = T["ps%d" % k], T["ta%d" % k], T["tb%d" % k], T["P%d" % k]
+        mm, vs = S["mm%d" % k], S["v%d" % k]
+        if first:
+            g.tensor.wait_ge(S.wl, 16)
+            g.tensor.wait_ge(S.wa, n_wa)
+            first = False
+        if k == 1:
+            if n_xa1:
+                g.tensor.wait_ge(S.xa1, n_xa1)
+            if n_xr:
+                g.tensor.wait_ge(S.xr, n_xr)
+        elif k == 2:
+            g.tensor.wait_ge(S.xa2, n_xa2)
+        else:
+            g.tensor.wait_ge(S.xl, 16)
+        for j in range(nm):
+            g.tensor.matmul(ps[:, j * wd:(j + 1) * wd], T.W[:, j * D:(j + 1) * D], T.X[:, c0:c0 + wd],
+                            True, True).then_inc(mm, 1)
+        g.vector.wait_ge(mm, nm)
+        g.vector.tensor_copy(ta[:, 0:2 * wd], ps[:, 0:2 * wd]).then_inc(vs, 1)
+        g.vector.wait_ge(vs, 1)
+        g.vector.tensor_tensor(tb[:, 0:2 * wd], ta[:, 0:2 * wd], ps[:, 2 * wd:4 * wd], AluOpType.max).then_inc(vs, 1)
+        g.vector.wait_ge(vs, 2)
+        g.vector.tensor_tensor(out[:, 0:wd], tb[:, 0:wd], tb[:, wd:2 * wd], AluOpType.max).then_inc(vs, 1)
+        if k < 3:
+            g.wait_ge(vs, 3)
+            items = []
+            for i, (r, bits) in enumerate(P["ret"][core][k - 1]):
+                li = P["lands"][r].index(core)
+                items.append((out[:, i * TK:(i + 1) * TK], [(r, T.LAND[:, li * TK:(li + 1) * TK])], bits,
+                              S["ra%d" % li]))
+            fused(items)
+    g.wait_ge(S.ls, sent[0])
+
+    parts = []
+    if is_host:
+        parts.append((T.P3[:, :], S.v3, 3))
+    for li, h in enumerate(P["lands"][core]):
+        bits = [b for wv in P["ret"][h] for r, b in wv if r == core][0]
+        parts.append((T.LAND[:, li * TK:(li + 1) * TK], S["ra%d" % li], len(bits)))
+    acc, sem, val = parts[0]
+    g.vector.wait_ge(sem, val)
+    for i, (ap, sem, val) in enumerate(parts[1:]):
+        g.vector.wait_ge(sem, val)
+        if i:
+            g.vector.wait_ge(S.vf, i)
+        out = T.Y[:, :] if i == len(parts) - 2 else T.TT[:, i * TK:(i + 1) * TK]
+        g.vector.tensor_tensor(out, acc, ap, AluOpType.max).then_inc(S.vf, 1)
+        acc = out
+    g.sync.wait_ge(S.vf, len(parts) - 1)
+    g.sync.dma_start(T.y[:, :], T.Y[:, :]).then_inc(S.st, 16)
+    g.sync.wait_ge(S.st, 16)

@@ -5,26 +5,26 @@ TK = 32
 D = 128
 
 SCRATCH = {
-    "W": ("sbuf", [128, 4 * D], "bfloat16"),
-    "X": ("sbuf", [128, 8 * TK], "bfloat16"),
+    "W": ("sbuf", [128, 12 * D], "bfloat16"),
+    "X": ("sbuf", [128, 4 * TK], "bfloat16"),
     "ps1": ("psum", [128, 512], "float32"),
     "ps2": ("psum", [128, 512], "float32"),
     "ps3": ("psum", [128, 512], "float32"),
-    "ta1": ("sbuf", [128, 256], "float32"),
-    "tb1": ("sbuf", [128, 256], "float32"),
-    "ta2": ("sbuf", [128, 256], "float32"),
-    "tb2": ("sbuf", [128, 256], "float32"),
-    "ta3": ("sbuf", [128, 256], "float32"),
-    "tb3": ("sbuf", [128, 256], "float32"),
-    "P1": ("sbuf", [128, 4 * TK], "bfloat16"),
-    "P2": ("sbuf", [128, 4 * TK], "bfloat16"),
-    "P3": ("sbuf", [128, TK], "bfloat16"),
-    "LAND": ("sbuf", [128, 4 * TK], "bfloat16"),
+    "ph0": ("psum", [128, 512], "float32"),
+    "ph1": ("psum", [128, 512], "float32"),
+    "u1": ("sbuf", [128, 256], "float32"),
+    "u2": ("sbuf", [128, 256], "float32"),
+    "P": ("sbuf", [128, 4 * TK], "bfloat16"),
+    "PO": ("sbuf", [128, TK], "bfloat16"),
+    "OF": ("sbuf", [128, TK], "float32"),
+    "TF": ("sbuf", [128, 4 * TK], "float32"),
+    "H": ("sbuf", [128, 2 * TK], "bfloat16"),
+    "LAND": ("sbuf", [128, 2 * TK], "bfloat16"),
     "TT": ("sbuf", [128, 4 * TK], "bfloat16"),
     "Y": ("sbuf", [128, TK], "bfloat16"),
 }
-SEMAPHORES = ["xl", "wl", "wa", "xr", "xa1", "xa2", "mm1", "mm2", "mm3", "v1", "v2", "v3",
-              "ra0", "ra1", "ra2", "ra3", "vf", "st", "ls"]
+SEMAPHORES = ["xl", "wl", "wa", "wr", "we", "xa", "h0", "h1", "mm1", "mm2", "ma0", "ma1", "ma2", "ma3", "mh0", "mh1",
+              "vs1", "vs2", "ra0", "ra1", "vf", "st", "ls"]
 
 
 def _bits(mask):
@@ -47,85 +47,72 @@ def _split(bits, n):
 
 def _plan(cores, topo):
     chip = topo.chip
+    ok = topo.may_write
     chips = []
     for c in cores:
         if chip(c) not in chips:
             chips.append(chip(c))
     mem = {ch: [c for c in cores if chip(c) == ch] for ch in chips}
-    hosts = {ch: [m for m in mem[ch] if any(topo.may_write(m, r) for r in cores if chip(r) != ch)] for ch in chips}
+    pos = {c: mem[chip(c)].index(c) for c in cores}
+    crowd = {c: sum(1 for m in mem[chip(c)] if topo.die(m) == topo.die(c)) for c in cores}
+    blocked = {ch: [r for r in cores if chip(r) != ch and not any(ok(r, m) for m in mem[ch])] for ch in chips}
+    pull = {c: [] for c in cores}
+    hard = {c: [] for c in cores}
+    wfar = {c: [] for c in cores}
+    fwd = {c: [] for c in cores}
     load = {c: 0 for c in cores}
-    nlate = {c: 0 for c in cores}
-    host, late = {}, {}
+    for ch in chips:
+        shut = blocked[ch]
+        if not shut:
+            continue
+        easy = [m for m in mem[ch] if all(ok(m, r) for r in shut)]
+        for k, m in enumerate(easy):
+            p = shut[k % len(shut)]
+            pull[p].append(m)
+            wfar[m].append(p)
+            load[m] += 1
+        for m in mem[ch]:
+            if m in easy:
+                continue
+            for r in shut:
+                q = min([q for q in mem[ch] if q != m and ok(q, r)], key=lambda q: (load[q], crowd[q], pos[q]))
+                hard[r].append((m, q))
+                fwd[q].append((m, r))
+                load[q] += 1
+    host = {}
+    guests = {c: [] for c in cores}
+    for ch in chips:
+        for r in blocked[ch]:
+            for p in blocked[ch]:
+                if p != r and any(chip(m) == ch for m in pull[p]):
+                    host[(r, chip(p))] = p
+                    guests[p].append(r)
     for ch in chips:
         todo = []
-        for i, r in enumerate(cores):
-            if chip(r) == ch:
+        for r in cores:
+            if chip(r) == ch or r in blocked[ch] or (r, ch) in host:
                 continue
-            back = [h for h in hosts[ch] if topo.may_write(h, r)]
-            direct = [h for h in back if topo.may_write(r, h)]
-            todo.append((1 if direct else 0, len(direct or back), i, r, direct or back))
-        for early, _n, _i, r, cand in sorted(todo):
-            h = min(cand, key=lambda c: (0 if early else nlate[c], load[c], cores.index(c)))
+            cand = [h for h in mem[ch] if ok(r, h) and ok(h, r)]
+            todo.append((len(cand), cores.index(r), r, cand))
+        for _n, _i, r, cand in sorted(todo):
+            room = [h for h in cand if (len(mem[ch]) + len(pull[h])) * (len(guests[h]) + 2) * TK <= 512]
+            h = min(room, key=lambda h: (len(guests[h]), topo.die(h) != topo.die(r), abs(pos[h] - pos[r])))
             host[(r, ch)] = h
-            late[(r, ch)] = not early
-            load[h] += 1
-            nlate[h] += 0 if early else 1
-    for r in cores:
-        ch = chip(r)
-        host[(r, ch)] = r if r in hosts[ch] else min(hosts[ch], key=lambda c: (load[c], cores.index(c)))
-        late[(r, ch)] = False
-    via = {}
-    for (r, ch), is_late in sorted(late.items()):
-        if not is_late:
-            continue
-        h, home = host[(r, ch)], host[(r, chip(r))]
-        cand = [q for q in mem[chip(r)] if q != r and topo.may_write(q, h)]
-        q = home if home in cand else min(cand, key=lambda c: (nlate[c], load[c], cores.index(c)))
-        via[(r, ch)] = q
-        load[q] += 1
-    wave1 = {c: [] for c in cores}
-    wave2 = {c: [] for c in cores}
-    relay = {c: {} for c in cores}
-    xdst = {c: [] for c in cores}
-    for r in cores:
-        for ch in chips:
-            q = via.get((r, ch))
-            if q is not None:
-                relay[q].setdefault(r, []).append(host[(r, ch)])
-                wave2[host[(r, ch)]].append(r)
-                if q not in xdst[r]:
-                    xdst[r].append(q)
-        for ch in chips:
-            h = host[(r, ch)]
-            if (r, ch) not in via and h != r:
-                wave1[h].append(r)
-                if h not in xdst[r]:
-                    xdst[r].append(h)
-    col = {}
-    for c in cores:
-        order = wave1[c] + wave2[c] + [c] + [r for r in relay[c] if r not in wave1[c]]
-        col[c] = {r: k for k, r in enumerate(order)}
-    lands = {r: [host[(r, chip(r))]] * (host[(r, chip(r))] != r) + [host[(r, ch)] for ch in chips if ch != chip(r)]
-             for r in cores}
-    needs = {r: any((r, ch) in via for ch in chips) for r in cores}
-    offb, onb, xbits, wbits, wdst, ret = {}, {}, {}, {}, {}, {}
+            guests[h].append(r)
+    xdst = {r: [host[(r, ch)] for ch in chips if (r, ch) in host] for r in cores}
+    passers = {m: [] for m in cores}
+    for q in cores:
+        for m, _r in fwd[q]:
+            if q not in passers[m]:
+                passers[m].append(q)
+    offb, onb = {}, {}
     for c in cores:
         far = [o for o in cores if chip(o) != chip(c)][0]
         near = [o for o in mem[chip(c)] if o != c][0]
         offb[c] = _bits(topo.mask(c, far))
         onb[c] = [b for b in _bits(topo.mask(c, near)) if b not in offb[c]]
-        xbits[c] = offb[c]
-        wbits[c] = (offb[c] + onb[c]) if needs[c] else (onb[c] or offb[c])
-        wdst[c] = [h for h in hosts[chip(c)] if h != c]
-        ret[c] = []
-        for wave in (wave1[c], wave2[c]):
-            off = [r for r in wave if chip(r) != chip(c)]
-            on = [r for r in wave if chip(r) == chip(c)]
-            eng = dict(zip(off, _split(offb[c], max(1, len(off)))))
-            eng.update(zip(on, _split(onb[c] or offb[c], max(1, len(on)))))
-            ret[c].append([(r, eng[r]) for r in wave])
-    return dict(mem=mem, hosts=hosts, wave1=wave1, wave2=wave2, relay=relay, xdst=xdst, col=col, lands=lands,
-                needs=needs, xbits=xbits, wbits=wbits, wdst=wdst, ret=ret)
+    return dict(mem=mem, pull=pull, hard=hard, wfar=wfar, fwd=fwd, guests=guests, xdst=xdst, passers=passers,
+                offb=offb, onb=onb)
 
 
 def rank_program(g, core, T, topo):
@@ -135,17 +122,19 @@ def rank_program(g, core, T, topo):
     P = _plan(cores, topo)
     S = T.sem
     mem = P["mem"][topo.chip(core)]
-    nm = len(mem)
-    is_host = core in P["hosts"][topo.chip(core)]
+    offb, onb = P["offb"], P["onb"]
     sent = [0]
 
-    def xslot(c, r):
-        k = P["col"][c][r]
-        return T.X[:, k * TK:(k + 1) * TK]
+    def worder(c):
+        return P["mem"][topo.chip(c)] + P["pull"][c] + [m for m, _q in P["hard"][c]]
 
-    def wslot(m):
-        k = mem.index(m)
+    def wslot(c, m):
+        k = worder(c).index(m)
         return T.W[:, k * D:(k + 1) * D]
+
+    def xslot(c, r):
+        k = (P["guests"][c] + [c]).index(r)
+        return T.X[:, k * TK:(k + 1) * TK]
 
     def ident(c):
         rid, pid, _se = topo.addr(c)
@@ -160,93 +149,169 @@ def rank_program(g, core, T, topo):
         g.remote_dma_fused(trs, local_sem=S.ls)
 
     g.sync.dma_start(xslot(core, core), T.x[:, :]).then_inc(S.xl, 16)
-    g.scalar.dma_start(wslot(core), T.w[:, :]).then_inc(S.wl, 16)
+    g.scalar.dma_start(wslot(core, core), T.w[:, :]).then_inc(S.wl, 16)
 
-    n_wa = sum(len(P["wbits"][m]) for m in mem if m != core) if is_host else 0
-    n_xr = sum(len(P["xbits"][s]) for s in cores if P["needs"][s] and core in P["xdst"][s])
-    n_xa1 = sum(len(P["xbits"][s]) for s in cores if not P["needs"][s] and core in P["xdst"][s])
-    n_xa2 = sum(len(P["xbits"][q]) for q in cores for r, hs in P["relay"][q].items() if core in hs)
+    n_wa = sum(len(onb[m]) for m in mem if m != core and not P["passers"][m])
+    n_wr = sum(len(offb[m]) if core in P["passers"][m] else len(onb[m])
+               for m in mem if m != core and P["passers"][m])
+    n_we = sum(len(offb[m]) for m in P["pull"][core])
+    n_xa = sum(len(offb[r]) for r in P["guests"][core])
 
     def send_x():
-        g.wait_ge(S.xl, 16)
-        fused([(xslot(core, core), [(c, xslot(c, core)) for c in P["xdst"][core]], P["xbits"][core],
-                S.xr if P["needs"][core] else S.xa1)])
+        if P["xdst"][core]:
+            g.wait_ge(S.xl, 16)
+            fused([(xslot(core, core), [(h, xslot(h, core)) for h in P["xdst"][core]], offb[core], S.xa)])
 
     def send_w():
         g.wait_ge(S.wl, 16)
-        fused([(wslot(core), [(c, wslot(core)) for c in P["wdst"][core]], P["wbits"][core], S.wa)])
-
-    x_rows = len(P["xdst"][core]) / len(P["xbits"][core])
-    w_rows = len(P["wdst"][core]) / len(P["wbits"][core])
-    if P["needs"][core] or x_rows >= w_rows:
-        send_x()
-        send_w()
-    else:
-        send_w()
-        send_x()
-    if P["relay"][core]:
-        g.wait_ge(S.xr, n_xr)
-        for r, hs in P["relay"][core].items():
-            fused([(xslot(core, r), [(h, xslot(h, r)) for h in hs], P["xbits"][core], S.xa2)])
-
-    waves = []
-    if is_host:
-        waves = [(1, P["wave1"][core]), (2, P["wave2"][core]), (3, [core])]
-    first = True
-    for k, wave in waves:
-        if not wave:
-            continue
-        wd = TK * len(wave)
-        c0 = P["col"][core][wave[0]] * TK
-        ps, ta, tb, out = T["ps%d" % k], T["ta%d" % k], T["tb%d" % k], T["P%d" % k]
-        mm, vs = S["mm%d" % k], S["v%d" % k]
-        if first:
-            g.tensor.wait_ge(S.wl, 16)
-            g.tensor.wait_ge(S.wa, n_wa)
-            first = False
-        if k == 1:
-            if n_xa1:
-                g.tensor.wait_ge(S.xa1, n_xa1)
-            if n_xr:
-                g.tensor.wait_ge(S.xr, n_xr)
-        elif k == 2:
-            g.tensor.wait_ge(S.xa2, n_xa2)
+        src = wslot(core, core)
+        items = []
+        if P["passers"][core]:
+            first = P["passers"][core]
+            rest = [m for m in mem if m != core and m not in first]
+            items.append((src, [(m, wslot(m, core)) for m in first], offb[core], S.wr))
+            if rest:
+                items.append((src, [(m, wslot(m, core)) for m in rest], onb[core], S.wr))
         else:
-            g.tensor.wait_ge(S.xl, 16)
+            items.append((src, [(m, wslot(m, core)) for m in mem if m != core], onb[core], S.wa))
+            if P["wfar"][core]:
+                items.append((src, [(p, wslot(p, core)) for p in P["wfar"][core]], offb[core], S.we))
+        fused(items)
+
+    if P["passers"][core]:
+        send_w()
+        send_x()
+    else:
+        send_x()
+        send_w()
+    for m, r in P["fwd"][core]:
+        g.wait_ge(S.wr, n_wr)
+        k = [o for o, _q in P["hard"][r]].index(m)
+        fused([(wslot(core, m), [(r, wslot(r, m))], offb[core], S["h%d" % k])])
+
+    guests = P["guests"][core]
+    ng = len(guests)
+    nm = len(mem)
+    npull = len(P["pull"][core])
+    own32 = bool(npull) and not guests and not P["xdst"][core]
+
+    def mms(ps, sem, w0, n, c0, wd):
+        for j in range(n):
+            g.tensor.matmul(ps[:, j * wd:(j + 1) * wd], T.W[:, (w0 + j) * D:(w0 + j + 1) * D], T.X[:, c0:c0 + wd],
+                            True, True).then_inc(sem, 1)
+
+    def reduce(ps, u, sem, n, wd, seeded, out):
+        cnt = [0]
+
+        def step(ins):
+            ins.then_inc(sem, 1)
+            cnt[0] += 1
+            g.vector.wait_ge(sem, cnt[0])
+
+        h = n // 2
+        keep = n - h
+        if seeded and n <= 2:
+            acc = u[:, keep * wd:(keep + 1) * wd]
+            for b in range(n):
+                step(g.vector.tensor_tensor(out if b == n - 1 else acc, acc, ps[:, b * wd:(b + 1) * wd], AluOpType.max))
+            return cnt[0]
+        step(g.vector.tensor_copy(u[:, 0:keep * wd], ps[:, 0:keep * wd]))
+        step(g.vector.tensor_tensor(u[:, 0:h * wd], u[:, 0:h * wd], ps[:, keep * wd:n * wd], AluOpType.max))
+        m_ = keep + (1 if seeded else 0)
+        while m_ > 1:
+            h = m_ // 2
+            step(g.vector.tensor_tensor(out if m_ == 2 else u[:, 0:h * wd], u[:, 0:h * wd],
+                                        u[:, (m_ - h) * wd:m_ * wd], AluOpType.max))
+            m_ -= h
+        return cnt[0]
+
+    g.tensor.wait_ge(S.wl, 16)
+    if n_xa:
+        g.tensor.wait_ge(S.xa, n_xa)
+    if n_wa:
+        g.tensor.wait_ge(S.wa, n_wa)
+    if n_wr:
+        g.tensor.wait_ge(S.wr, n_wr)
+    if npull:
+        wd = TK * (ng + 1)
+        keep2 = npull - npull // 2
+        g.tensor.wait_ge(S.xl, 16)
+        mms(T.ps1, S.mm1, 0, nm, 0, wd)
+        g.tensor.wait_ge(S.we, n_we)
+        mms(T.ps2, S.mm2, nm, npull, 0, wd)
+        g.vector.wait_ge(S.mm1, nm)
+        reduce(T.ps1, T.u1, S.vs1, nm, wd, False, T.u2[:, keep2 * wd:(keep2 + 1) * wd])
+        g.vector.wait_ge(S.mm2, npull)
+        ready = (S.vs2, reduce(T.ps2, T.u2, S.vs2, npull, wd, True, T.OF[:, 0:wd] if own32 else T.P[:, 0:wd]))
+        own = T.OF[:, 0:TK] if own32 else T.P[:, wd - TK:wd]
+    else:
+        wd = TK * ng
+        banks = [T.ps1, T.ph0, T.ph1, T.ps3]
         for j in range(nm):
-            g.tensor.matmul(ps[:, j * wd:(j + 1) * wd], T.W[:, j * D:(j + 1) * D], T.X[:, c0:c0 + wd],
-                            True, True).then_inc(mm, 1)
-        g.vector.wait_ge(mm, nm)
-        g.vector.tensor_copy(ta[:, 0:2 * wd], ps[:, 0:2 * wd]).then_inc(vs, 1)
-        g.vector.wait_ge(vs, 1)
-        g.vector.tensor_tensor(tb[:, 0:2 * wd], ta[:, 0:2 * wd], ps[:, 2 * wd:4 * wd], AluOpType.max).then_inc(vs, 1)
-        g.vector.wait_ge(vs, 2)
-        g.vector.tensor_tensor(out[:, 0:wd], tb[:, 0:wd], tb[:, wd:2 * wd], AluOpType.max).then_inc(vs, 1)
-        if k < 3:
-            g.wait_ge(vs, 3)
-            items = []
-            for i, (r, bits) in enumerate(P["ret"][core][k - 1]):
-                li = P["lands"][r].index(core)
-                items.append((out[:, i * TK:(i + 1) * TK], [(r, T.LAND[:, li * TK:(li + 1) * TK])], bits,
-                              S["ra%d" % li]))
-            fused(items)
+            g.tensor.matmul(banks[j][:, 0:wd], T.W[:, j * D:(j + 1) * D], T.X[:, 0:wd],
+                            True, True).then_inc(S["ma%d" % j], 1)
+        for j in range(nm):
+            g.vector.wait_ge(S["ma%d" % j], 1)
+            if j == 0:
+                ins = g.vector.tensor_copy(T.u1[:, 0:wd], banks[0][:, 0:wd])
+            else:
+                ins = g.vector.tensor_tensor(T.P[:, 0:wd] if j == nm - 1 else T.u1[:, 0:wd], T.u1[:, 0:wd],
+                                             banks[j][:, 0:wd], AluOpType.max)
+            ins.then_inc(S.vs1, 1)
+            g.vector.wait_ge(S.vs1, j + 1)
+        ready = (S.vs1, nm)
+        g.tensor.wait_ge(S.xl, 16)
+        mms(T.ps2, S.mm2, 0, nm, wd, TK)
+        g.vector.wait_ge(S.mm2, nm)
+        reduce(T.ps2, T.u2, S.vs2, nm, TK, False, T.PO[:, 0:TK])
+        own = T.PO[:, 0:TK]
+    for k, (m, q) in enumerate(P["hard"][core]):
+        g.tensor.wait_ge(S["h%d" % k], len(offb[q]))
+        g.tensor.matmul(T["ph%d" % k][:, 0:TK], wslot(core, m), xslot(core, core), True, True).then_inc(S["mh%d" % k], 1)
+
+    if guests:
+        g.wait_ge(ready[0], ready[1])
+        items = []
+        for i, (r, bits) in enumerate(zip(guests, _split(offb[core], ng))):
+            li = P["xdst"][r].index(core)
+            items.append((T.P[:, i * TK:(i + 1) * TK], [(r, T.LAND[:, li * TK:(li + 1) * TK])], bits, S["ra%d" % li]))
+        fused(items)
     g.wait_ge(S.ls, sent[0])
 
-    parts = []
-    if is_host:
-        parts.append((T.P3[:, :], S.v3, 3))
-    for li, h in enumerate(P["lands"][core]):
-        bits = [b for wv in P["ret"][h] for r, b in wv if r == core][0]
-        parts.append((T.LAND[:, li * TK:(li + 1) * TK], S["ra%d" % li], len(bits)))
-    acc, sem, val = parts[0]
-    g.vector.wait_ge(sem, val)
-    for i, (ap, sem, val) in enumerate(parts[1:]):
-        g.vector.wait_ge(sem, val)
-        if i:
-            g.vector.wait_ge(S.vf, i)
-        out = T.Y[:, :] if i == len(parts) - 2 else T.TT[:, i * TK:(i + 1) * TK]
-        g.vector.tensor_tensor(out, acc, ap, AluOpType.max).then_inc(S.vf, 1)
+    todo = []
+    for k in range(len(P["hard"][core])):
+        todo.append(("late", k, 1))
+    lands = []
+    for li, hc in enumerate(P["xdst"][core]):
+        gl = P["guests"][hc]
+        bits = _split(offb[hc], len(gl))[gl.index(core)]
+        lands.append((0 if topo.same_plane(topo.chip(core), topo.chip(hc)) else 1, li, len(bits)))
+    for _far, li, val in sorted(lands):
+        todo.append(("land", li, val))
+    acc = own
+    nf = [0]
+
+    def fstep(ins):
+        ins.then_inc(S.vf, 1)
+        nf[0] += 1
+
+    for i, (kind, k, val) in enumerate(todo):
+        last = i == len(todo) - 1
+        out = T.Y[:, :] if last else (T.TF if own32 else T.TT)[:, i * TK:(i + 1) * TK]
+        if kind == "land":
+            g.vector.wait_ge(S["ra%d" % k], val)
+            other = T.LAND[:, k * TK:(k + 1) * TK]
+        elif own32:
+            g.vector.wait_ge(S["mh%d" % k], val)
+            other = T["ph%d" % k][:, 0:TK]
+        else:
+            g.vector.wait_ge(S["mh%d" % k], val)
+            other = T.H[:, k * TK:(k + 1) * TK]
+            fstep(g.vector.tensor_copy(other, T["ph%d" % k][:, 0:TK]))
+        if nf[0]:
+            g.vector.wait_ge(S.vf, nf[0])
+        fstep(g.vector.tensor_tensor(out, acc, other, AluOpType.max))
         acc = out
-    g.sync.wait_ge(S.vf, len(parts) - 1)
+    g.sync.wait_ge(S.vf, nf[0])
     g.sync.dma_start(T.y[:, :], T.Y[:, :]).then_inc(S.st, 16)
     g.sync.wait_ge(S.st, 16)

from concourse.bass import DstId, RemoteDMATransfer
from concourse.mybir import AluOpType

TK = 32
D = 128

SCRATCH = {
    "W": ("sbuf", [128, 12 * D], "bfloat16"),
    "X": ("sbuf", [128, 4 * TK], "bfloat16"),
    "ps1": ("psum", [128, 512], "float32"),
    "ps2": ("psum", [128, 512], "float32"),
    "ps3": ("psum", [128, 512], "float32"),
    "ph0": ("psum", [128, 512], "float32"),
    "ph1": ("psum", [128, 512], "float32"),
    "u1": ("sbuf", [128, 256], "float32"),
    "u2": ("sbuf", [128, 256], "float32"),
    "P": ("sbuf", [128, 4 * TK], "bfloat16"),
    "PO": ("sbuf", [128, TK], "bfloat16"),
    "OF": ("sbuf", [128, TK], "float32"),
    "TF": ("sbuf", [128, 4 * TK], "float32"),
    "H": ("sbuf", [128, 2 * TK], "bfloat16"),
    "LAND": ("sbuf", [128, 2 * TK], "bfloat16"),
    "TT": ("sbuf", [128, 4 * TK], "bfloat16"),
    "Y": ("sbuf", [128, TK], "bfloat16"),
}
SEMAPHORES = ["xl", "wl", "wa", "wr", "we", "xa", "h0", "h1", "mm1", "mm2", "ma0", "ma1", "ma2", "ma3", "mh0", "mh1",
              "vs1", "vs2", "ra0", "ra1", "vf", "st", "ls"]


def _bits(mask):
    return [i for i in range(mask.bit_length()) if (mask >> i) & 1]


def _mask(bits):
    m = 0
    for b in bits:
        m |= 1 << b
    return m


def _split(bits, n):
    k = 1
    while 2 * k * n <= len(bits):
        k *= 2
    return [bits[i * k:(i + 1) * k] for i in range(n)]


def _plan(cores, topo):
    chip = topo.chip
    ok = topo.may_write
    chips = []
    for c in cores:
        if chip(c) not in chips:
            chips.append(chip(c))
    mem = {ch: [c for c in cores if chip(c) == ch] for ch in chips}
    pos = {c: mem[chip(c)].index(c) for c in cores}
    crowd = {c: sum(1 for m in mem[chip(c)] if topo.die(m) == topo.die(c)) for c in cores}
    blocked = {ch: [r for r in cores if chip(r) != ch and not any(ok(r, m) for m in mem[ch])] for ch in chips}
    pull = {c: [] for c in cores}
    hard = {c: [] for c in cores}
    wfar = {c: [] for c in cores}
    fwd = {c: [] for c in cores}
    load = {c: 0 for c in cores}
    for ch in chips:
        shut = blocked[ch]
        if not shut:
            continue
        easy = [m for m in mem[ch] if all(ok(m, r) for r in shut)]
        for k, m in enumerate(easy):
            p = shut[k % len(shut)]
            pull[p].append(m)
            wfar[m].append(p)
            load[m] += 1
        for m in mem[ch]:
            if m in easy:
                continue
            for r in shut:
                q = min([q for q in mem[ch] if q != m and ok(q, r)], key=lambda q: (load[q], crowd[q], pos[q]))
                hard[r].append((m, q))
                fwd[q].append((m, r))
                load[q] += 1
    host = {}
    guests = {c: [] for c in cores}
    for ch in chips:
        for r in blocked[ch]:
            for p in blocked[ch]:
                if p != r and any(chip(m) == ch for m in pull[p]):
                    host[(r, chip(p))] = p
                    guests[p].append(r)
    for ch in chips:
        todo = []
        for r in cores:
            if chip(r) == ch or r in blocked[ch] or (r, ch) in host:
                continue
            cand = [h for h in mem[ch] if ok(r, h) and ok(h, r)]
            todo.append((len(cand), cores.index(r), r, cand))
        for _n, _i, r, cand in sorted(todo):
            room = [h for h in cand if (len(mem[ch]) + len(pull[h])) * (len(guests[h]) + 2) * TK <= 512]
            h = min(room, key=lambda h: (len(guests[h]), topo.die(h) != topo.die(r), abs(pos[h] - pos[r])))
            host[(r, ch)] = h
            guests[h].append(r)
    xdst = {r: [host[(r, ch)] for ch in chips if (r, ch) in host] for r in cores}
    passers = {m: [] for m in cores}
    for q in cores:
        for m, _r in fwd[q]:
            if q not in passers[m]:
                passers[m].append(q)
    offb, onb = {}, {}
    for c in cores:
        far = [o for o in cores if chip(o) != chip(c)][0]
        near = [o for o in mem[chip(c)] if o != c][0]
        offb[c] = _bits(topo.mask(c, far))
        onb[c] = [b for b in _bits(topo.mask(c, near)) if b not in offb[c]]
    return dict(mem=mem, pull=pull, hard=hard, wfar=wfar, fwd=fwd, guests=guests, xdst=xdst, passers=passers,
                offb=offb, onb=onb)


def rank_program(g, core, T, topo):
    if T.rank_of(core) is None:
        return
    cores = list(T.cores)
    P = _plan(cores, topo)
    S = T.sem
    mem = P["mem"][topo.chip(core)]
    offb, onb = P["offb"], P["onb"]
    sent = [0]

    def worder(c):
        return P["mem"][topo.chip(c)] + P["pull"][c] + [m for m, _q in P["hard"][c]]

    def wslot(c, m):
        k = worder(c).index(m)
        return T.W[:, k * D:(k + 1) * D]

    def xslot(c, r):
        k = (P["guests"][c] + [c]).index(r)
        return T.X[:, k * TK:(k + 1) * TK]

    def ident(c):
        rid, pid, _se = topo.addr(c)
        return DstId(rid=rid, pnc=pid)

    def fused(items):
        trs = []
        for src, dl, bits, sem in items:
            trs.append(RemoteDMATransfer(dst_ids=[ident(c) for c, _a in dl], dma_engine_mask=_mask(bits),
                                         remote_sem=sem, srcs=[src], dsts=[a for _c, a in dl], alu_op=0))
            sent[0] += len(bits)
        g.remote_dma_fused(trs, local_sem=S.ls)

    g.sync.dma_start(xslot(core, core), T.x[:, :]).then_inc(S.xl, 16)
    g.scalar.dma_start(wslot(core, core), T.w[:, :]).then_inc(S.wl, 16)

    n_wa = sum(len(onb[m]) for m in mem if m != core and not P["passers"][m])
    n_wr = sum(len(offb[m]) if core in P["passers"][m] else len(onb[m])
               for m in mem if m != core and P["passers"][m])
    n_we = sum(len(offb[m]) for m in P["pull"][core])
    n_xa = sum(len(offb[r]) for r in P["guests"][core])

    def send_x():
        if P["xdst"][core]:
            g.wait_ge(S.xl, 16)
            fused([(xslot(core, core), [(h, xslot(h, core)) for h in P["xdst"][core]], offb[core], S.xa)])

    def send_w():
        g.wait_ge(S.wl, 16)
        src = wslot(core, core)
        items = []
        if P["passers"][core]:
            first = P["passers"][core]
            rest = [m for m in mem if m != core and m not in first]
            items.append((src, [(m, wslot(m, core)) for m in first], offb[core], S.wr))
            if rest:
                items.append((src, [(m, wslot(m, core)) for m in rest], onb[core], S.wr))
        else:
            items.append((src, [(m, wslot(m, core)) for m in mem if m != core], onb[core], S.wa))
            if P["wfar"][core]:
                items.append((src, [(p, wslot(p, core)) for p in P["wfar"][core]], offb[core], S.we))
        fused(items)

    if P["passers"][core]:
        send_w()
        send_x()
    else:
        send_x()
        send_w()
    for m, r in P["fwd"][core]:
        g.wait_ge(S.wr, n_wr)
        k = [o for o, _q in P["hard"][r]].index(m)
        fused([(wslot(core, m), [(r, wslot(r, m))], offb[core], S["h%d" % k])])

    guests = P["guests"][core]
    ng = len(guests)
    nm = len(mem)
    npull = len(P["pull"][core])
    own32 = bool(npull) and not guests and not P["xdst"][core]

    def mms(ps, sem, w0, n, c0, wd):
        for j in range(n):
            g.tensor.matmul(ps[:, j * wd:(j + 1) * wd], T.W[:, (w0 + j) * D:(w0 + j + 1) * D], T.X[:, c0:c0 + wd],
                            True, True).then_inc(sem, 1)

    def reduce(ps, u, sem, n, wd, seeded, out):
        cnt = [0]

        def step(ins):
            ins.then_inc(sem, 1)
            cnt[0] += 1
            g.vector.wait_ge(sem, cnt[0])

        h = n // 2
        keep = n - h
        if seeded and n <= 2:
            acc = u[:, keep * wd:(keep + 1) * wd]
            for b in range(n):
                step(g.vector.tensor_tensor(out if b == n - 1 else acc, acc, ps[:, b * wd:(b + 1) * wd], AluOpType.max))
            return cnt[0]
        step(g.vector.tensor_copy(u[:, 0:keep * wd], ps[:, 0:keep * wd]))
        step(g.vector.tensor_tensor(u[:, 0:h * wd], u[:, 0:h * wd], ps[:, keep * wd:n * wd], AluOpType.max))
        m_ = keep + (1 if seeded else 0)
        while m_ > 1:
            h = m_ // 2
            step(g.vector.tensor_tensor(out if m_ == 2 else u[:, 0:h * wd], u[:, 0:h * wd],
                                        u[:, (m_ - h) * wd:m_ * wd], AluOpType.max))
            m_ -= h
        return cnt[0]

    g.tensor.wait_ge(S.wl, 16)
    if n_xa:
        g.tensor.wait_ge(S.xa, n_xa)
    if n_wa:
        g.tensor.wait_ge(S.wa, n_wa)
    if n_wr:
        g.tensor.wait_ge(S.wr, n_wr)
    if npull:
        wd = TK * (ng + 1)
        keep2 = npull - npull // 2
        g.tensor.wait_ge(S.xl, 16)
        mms(T.ps1, S.mm1, 0, nm, 0, wd)
        g.tensor.wait_ge(S.we, n_we)
        mms(T.ps2, S.mm2, nm, npull, 0, wd)
        g.vector.wait_ge(S.mm1, nm)
        reduce(T.ps1, T.u1, S.vs1, nm, wd, False, T.u2[:, keep2 * wd:(keep2 + 1) * wd])
        g.vector.wait_ge(S.mm2, npull)
        ready = (S.vs2, reduce(T.ps2, T.u2, S.vs2, npull, wd, True, T.OF[:, 0:wd] if own32 else T.P[:, 0:wd]))
        own = T.OF[:, 0:TK] if own32 else T.P[:, wd - TK:wd]
    else:
        wd = TK * ng
        banks = [T.ps1, T.ph0, T.ph1, T.ps3]
        for j in range(nm):
            g.tensor.matmul(banks[j][:, 0:wd], T.W[:, j * D:(j + 1) * D], T.X[:, 0:wd],
                            True, True).then_inc(S["ma%d" % j], 1)
        for j in range(nm):
            g.vector.wait_ge(S["ma%d" % j], 1)
            if j == 0:
                ins = g.vector.tensor_copy(T.u1[:, 0:wd], banks[0][:, 0:wd])
            else:
                ins = g.vector.tensor_tensor(T.P[:, 0:wd] if j == nm - 1 else T.u1[:, 0:wd], T.u1[:, 0:wd],
                                             banks[j][:, 0:wd], AluOpType.max)
            ins.then_inc(S.vs1, 1)
            g.vector.wait_ge(S.vs1, j + 1)
        ready = (S.vs1, nm)
        g.tensor.wait_ge(S.xl, 16)
        mms(T.ps2, S.mm2, 0, nm, wd, TK)
        g.vector.wait_ge(S.mm2, nm)
        reduce(T.ps2, T.u2, S.vs2, nm, TK, False, T.PO[:, 0:TK])
        own = T.PO[:, 0:TK]
    for k, (m, q) in enumerate(P["hard"][core]):
        g.tensor.wait_ge(S["h%d" % k], len(offb[q]))
        g.tensor.matmul(T["ph%d" % k][:, 0:TK], wslot(core, m), xslot(core, core), True, True).then_inc(S["mh%d" % k], 1)

    if guests:
        g.wait_ge(ready[0], ready[1])
        items = []
        for i, (r, bits) in enumerate(zip(guests, _split(offb[core], ng))):
            li = P["xdst"][r].index(core)
            items.append((T.P[:, i * TK:(i + 1) * TK], [(r, T.LAND[:, li * TK:(li + 1) * TK])], bits, S["ra%d" % li]))
        fused(items)
    g.wait_ge(S.ls, sent[0])

    todo = []
    for k in range(len(P["hard"][core])):
        todo.append(("late", k, 1))
    lands = []
    for li, hc in enumerate(P["xdst"][core]):
        gl = P["guests"][hc]
        bits = _split(offb[hc], len(gl))[gl.index(core)]
        lands.append((0 if topo.same_plane(topo.chip(core), topo.chip(hc)) else 1, li, len(bits)))
    for _far, li, val in sorted(lands):
        todo.append(("land", li, val))
    acc = own
    nf = [0]

    def fstep(ins):
        ins.then_inc(S.vf, 1)
        nf[0] += 1

    for i, (kind, k, val) in enumerate(todo):
        last = i == len(todo) - 1
        out = T.Y[:, :] if last else (T.TF if own32 else T.TT)[:, i * TK:(i + 1) * TK]
        if kind == "land":
            g.vector.wait_ge(S["ra%d" % k], val)
            other = T.LAND[:, k * TK:(k + 1) * TK]
        elif own32:
            g.vector.wait_ge(S["mh%d" % k], val)
            other = T["ph%d" % k][:, 0:TK]
        else:
            g.vector.wait_ge(S["mh%d" % k], val)
            other = T.H[:, k * TK:(k + 1) * TK]
            fstep(g.vector.tensor_copy(other, T["ph%d" % k][:, 0:TK]))
        if nf[0]:
            g.vector.wait_ge(S.vf, nf[0])
        fstep(g.vector.tensor_tensor(out, acc, other, AluOpType.max))
        acc = out
    g.sync.wait_ge(S.vf, nf[0])
    g.sync.dma_start(T.y[:, :], T.Y[:, :]).then_inc(S.st, 16)
    g.sync.wait_ge(S.st, 16)
